import numpy as np
import ml_dtypes


def mxq(x, axis, fmt="e4m3"):
    dtype, down = {"e4m3": (ml_dtypes.float8_e4m3fn, 7), "e5m2": (ml_dtypes.float8_e5m2, 14)}[fmt]
    v = np.moveaxis(np.asarray(x, np.float32).astype(ml_dtypes.bfloat16).astype(np.float64), axis, -1)
    blocks = v.reshape(v.shape[:-1] + (-1, 32))
    amax = np.abs(blocks).max(-1, keepdims=True)
    byte = np.maximum(np.where(amax > 0, np.frexp(amax)[1] - 1 + 127, 0) - down, 1)
    scale = np.exp2(byte - 127.0)
    codes = (blocks / scale).astype(np.float32).astype(dtype).astype(np.float64)
    return np.moveaxis((codes * scale).reshape(v.shape), -1, axis)


WIDE = False


def mx_kscale(k):
    if not WIDE:
        return np.ones(k)
    levels = np.array([10, -10, 5, -5, 0])
    if k % 512:
        return np.exp2(np.random.permutation(np.resize(levels, k // 32))).repeat(32)
    a = np.empty((k // 512, 16))
    for p in range(k // 512):
        a[p, :8] = np.random.permutation(np.resize(levels, 8))
        for g in range(8):
            far = levels[np.abs(levels - a[p, g]) >= 10]
            a[p, g + 8] = far[np.random.randint(len(far))]
    return np.exp2(a.ravel()).repeat(32)


def f64(x):
    return np.asarray(x).astype(np.float64)


def striped(idx):
    return np.tile(np.asarray(idx).reshape(-1, 16).T, (8, 1)).astype(np.uint16)


def unstriped(offs):
    return offs[:16].T.reshape(-1).astype(np.int64)


E2M1 = np.array([0.0, 0.5, 1.0, 1.5, 2.0, 3.0, 4.0, 6.0, -0.0, -0.5, -1.0, -1.5, -2.0, -3.0, -4.0, -6.0])


def pack_weight(w, fmt):
    k, n = w.shape
    w = f64(np.asarray(w, np.float32).astype(ml_dtypes.bfloat16)).reshape(k // 32, 32, n)
    amax = np.abs(w).max(1)
    if fmt == "e4m3":
        byte = np.frexp(amax)[1] - 1 + 127 - 7
    else:
        mant, ex = np.frexp(amax / 6.0)
        byte = np.where(mant > 0.5, ex, ex - 1) + 127
    byte = np.clip(np.where(amax > 0, byte, 1), 1, 254)
    scaled = (w * np.exp2(127.0 - byte)[:, None, :]).reshape(k, n).astype(np.float32)
    by_word = np.ascontiguousarray(scaled.reshape(k // 512, 128, 4, n).transpose(0, 1, 3, 2))
    if fmt == "e4m3":
        words = by_word.astype(ml_dtypes.float8_e4m3fn).view(np.uint8)
    else:
        c = by_word.astype(ml_dtypes.float4_e2m1fn).view(np.uint8) & 0xF
        words = (c[..., 0::2] | (c[..., 1::2] << 4)).reshape(k // 512, 128, 2 * n)
    return np.ascontiguousarray(words), np.ascontiguousarray(byte.astype(np.uint8).reshape(k // 512, 16, n))


def unpack_weight(words, scales, fmt):
    g, _, n = scales.shape
    words = np.ascontiguousarray(words).reshape(g, 128, n, -1)
    if fmt == "e4m3":
        vals = words.view(ml_dtypes.float8_e4m3fn).astype(np.float64)
    else:
        nib = np.empty((g, 128, n, 4), np.uint8)
        nib[..., 0::2] = words & 0xF
        nib[..., 1::2] = words >> 4
        vals = E2M1[nib]
    vals = vals * np.repeat(np.exp2(scales.astype(np.float64) - 127.0), 8, axis=1)[..., None]
    return vals.transpose(0, 1, 3, 2).reshape(g * 512, n)


def sigmoid(v):
    return 1.0 / (1.0 + np.exp(-v))


D, E, T, I, Q = 512, 512, 1024, 256, 512


def setup_inputs():
    n = np.random.standard_normal
    idx = np.random.permutation(T)[:I]
    fd = mx_kscale(D)
    fq = mx_kscale(Q)
    keysp = pack_weight(n((D, T)) / fd[:, None], "e4m3")
    return {
        "query": (n((D, Q)) * 0.8 / np.sqrt(D) * fd[:, None]).astype(np.float32),
        "keys_words": keysp[0],
        "keys_scales": keysp[1],
        "share": (np.random.uniform(0.2, 0.8, (Q, 1))).astype(np.float32),
        "qs": (np.random.uniform(2.0, 8.0, (Q, 1)) * fq[:, None]).astype(np.float32),
        "grows": (n((Q, E)) / fq[:, None]).astype(np.float32),
        "old": (n((E, T)) * 2.0).astype(np.float32),
        "fade": (np.random.uniform(0.5, 1.0, (1, T))).astype(np.float32),
        "offs": striped(idx),
    }


def reference(query, keys_words, keys_scales, share, qs, grows, old, fade, offs):
    idx = unstriped(offs)
    keysu = unpack_weight(keys_words, keys_scales, "e4m3")
    queryq = mxq(f64(query), 0, "e4m3")
    keysidxg = keysu[:, idx]
    a = queryq.T @ keysidxg
    e0 = np.exp(a)
    s0 = sigmoid(a)
    p = e0 * f64(share) + s0 * (1.0 - f64(share)) * 3.0
    z = np.sum(p, axis=1, keepdims=True)
    w = p / z
    wq = w * f64(qs)
    growsq = mxq(f64(grows), 0, "e4m3")
    wqq = mxq(wq, 0, "e4m3")
    gv = growsq.T @ wqq
    gf = np.zeros((E, T))
    gf[:, idx] = gv
    y = f64(old) * f64(fade) + gf
    return y

@@ -1,0 +1,211 @@
+from contextlib import ExitStack
+
+import concourse.mybir as mybir
+from concourse.masks import make_identity
+
+D, E, T, I, Q = 512, 512, 1024, 256, 512
+FLOPS = 2 * D * Q * I + 2 * Q * E * I
+
+F32 = mybir.dt.float32
+BF16 = mybir.dt.bfloat16
+I32 = mybir.dt.int32
+U32 = mybir.dt.uint32
+U16 = mybir.dt.uint16
+U8 = mybir.dt.uint8
+FP8X4 = mybir.dt.float8_e4m3fn_x4
+ACT = mybir.ActivationFunctionType
+ALU = mybir.AluOpType
+
+P = 128
+PACK = 4
+BANK = 512
+QUERY_SPLIT = 84
+
+
+def tile_attend_bmixedparts_v_kernel(tc, query, keys_words, keys_scales, share, qs, grows, old, fade, offs, out):
+    nc = tc.nc
+    tiles_e = E // P
+    with ExitStack() as ctx:
+        keep = ctx.enter_context(tc.tile_pool(name="keep", bufs=1))
+        psum = ctx.enter_context(tc.psum_pool(name="psum", bufs=1))
+
+        offsets = keep.tile([P, I // 16], U16, name="offsets")
+        nc.sync.dma_start(offsets[:], offs)
+
+        pool_words = keep.tile([P, T], U32, name="pool_words", align_bytes=64)
+        pool_scales = keep.tile([P, T], U8, name="pool_scales", align_bytes=64)
+        fade_rows = keep.tile([P, P], F32, name="fade_rows")
+        nc.gpsimd.memset(pool_scales[:].bitcast(I32), 0)
+        nc.gpsimd.memset(fade_rows[:], 0.0)
+
+        nc.sync.dma_start(pool_words[:].bitcast(I32), keys_words[0].rearrange("p n t -> p (n t)").bitcast(I32))
+        for quad in range(4):
+            nc.sync.dma_start(
+                pool_scales[32 * quad : 32 * quad + 4, :].bitcast(I32),
+                keys_scales[0, 4 * quad : 4 * quad + 4, :].bitcast(I32),
+            )
+        nc.sync.dma_start(fade_rows[0 : T // P, :], fade.rearrange("o (k n) -> (o k) n", n=P))
+        query_raw = keep.tile([P, PACK, Q], F32, name="query_raw")
+        nc.sync.dma_start(query_raw[:], query.rearrange("(p j) q -> p j q", j=PACK))
+        share_col = keep.tile([P, PACK], F32, name="share_col")
+        qs_col = keep.tile([P, PACK], F32, name="qs_col")
+        nc.sync.dma_start(share_col[:], share.rearrange("(p r) o -> p (r o)", r=PACK))
+        nc.sync.dma_start(qs_col[:], qs.rearrange("(p r) o -> p (r o)", r=PACK))
+
+        olds = [keep.tile([P, T], F32, name=f"olds{m}") for m in range(tiles_e)]
+        grows_raw = keep.tile([P, PACK, E], F32, name="grows_raw")
+        for m in range(2):
+            nc.sync.dma_start(olds[m][:], old[m * P : (m + 1) * P, :])
+        nc.sync.dma_start(grows_raw[:], grows.rearrange("(p j) e -> p j e", j=PACK))
+        for m in range(2, tiles_e):
+            nc.sync.dma_start(olds[m][:], old[m * P : (m + 1) * P, :])
+
+        identity = keep.tile([P, P], F32, name="identity")
+        make_identity(nc, identity[:])
+        placed = [keep.tile([P, T], F32, name=f"placed{m}") for m in range(tiles_e)]
+        for m in range(tiles_e):
+            nc.vector.memset(placed[m][:], 0.0)
+
+        rest_col = keep.tile([P, PACK], F32, name="rest_col")
+        nc.scalar.activation(rest_col[:], share_col[:], ACT.Copy, bias=3.0, scale=-3.0)
+
+        fade_turned = psum.tile([P, P], F32, name="fade_turned")
+        nc.tensor.transpose(fade_turned[:], fade_rows[:], identity[:])
+        fade_cols = keep.tile([P, T // P], F32, name="fade_cols")
+        nc.scalar.copy(fade_cols[:], fade_turned[:, 0 : T // P])
+        fade_wide = [psum.tile([P, BANK], F32, name=f"fade_wide{h}") for h in range(T // BANK)]
+        for k in range(T // P):
+            nc.tensor.transpose(
+                fade_wide[k // 4][:, (k % 4) * P : (k % 4 + 1) * P],
+                fade_cols[:, k : k + 1].to_broadcast([P, P]),
+                identity[:],
+            )
+
+        key_words = keep.tile([P, I], U32, name="key_words", align_bytes=64)
+        key_scales = keep.tile([P, I], U8, name="key_scales", align_bytes=64)
+        nc.vector.tensor_copy(key_words[:], pool_words[:].indirect(offsets[:]))
+        nc.vector.tensor_copy(key_scales[:], pool_scales[:].indirect(offsets[:]))
+
+        query_bf = keep.tile([P, PACK, P, PACK], BF16, name="query_bf", align_bytes=64)
+        dealt_out = query_bf[:].rearrange("p r s j -> p s j r")
+        dealt_in = query_raw[:].rearrange("p j (s r) -> p s j r", r=PACK)
+        nc.vector.tensor_copy(dealt_out[:, 0:QUERY_SPLIT], dealt_in[:, 0:QUERY_SPLIT])
+        nc.scalar.copy(dealt_out[:, QUERY_SPLIT:P], dealt_in[:, QUERY_SPLIT:P])
+
+        query_codes = keep.tile([P, Q], U32, name="query_codes", align_bytes=64)
+        query_scales = keep.tile([P, Q], U8, name="query_scales", align_bytes=64)
+        scores = []
+        for r in range(PACK):
+            cols = slice(r * P, (r + 1) * P)
+            nc.vector.quantize_mx(
+                out=query_codes[:, cols].bitcast(FP8X4),
+                scales=query_scales[:, cols],
+                in_=query_bf[:, r].rearrange("p s j -> p (s j)"),
+            )
+            score = psum.tile([P, I], F32, name=f"score{r}", tag=f"bank{r}")
+            nc.tensor.matmul_mx(
+                out=score[:],
+                lhsT=query_codes[:, cols].bitcast(FP8X4),
+                lhsT_scale=query_scales[:, cols],
+                rhs=key_words[:].bitcast(FP8X4),
+                rhs_scale=key_scales[:],
+                start=True,
+                stop=True,
+            )
+            scores.append(score)
+
+        exps = [keep.tile([P, I], F32, name=f"exps{r}") for r in range(PACK)]
+        shared = [keep.tile([P, I], F32, name=f"shared{r}") for r in range(PACK)]
+        sigs = [keep.tile([P, I], F32, name=f"sigs{r}") for r in range(PACK)]
+        parts = [keep.tile([P, I], F32, name=f"parts{r}") for r in range(PACK)]
+        sums = [keep.tile([P, 1], F32, name=f"sums{r}") for r in range(PACK)]
+        inverse = [keep.tile([P, 1], F32, name=f"inverse{r}") for r in range(PACK)]
+        weights = keep.tile([P, PACK, I], BF16, name="weights")
+        for r in range(PACK):
+            nc.scalar.activation(exps[r][:], scores[r][:], ACT.Exp)
+        for r in range(PACK):
+            nc.scalar.activation(sigs[r][:], scores[r][:], ACT.Sigmoid)
+        for r in range(PACK):
+            nc.vector.tensor_scalar(shared[r][:], exps[r][:], share_col[:, r : r + 1], None, ALU.mult)
+
+        def fade_tile(m, result):
+            for h in range(T // BANK):
+                cols = slice(h * BANK, (h + 1) * BANK)
+                nc.vector.tensor_tensor(result[:, cols], olds[m][:, cols], fade_wide[h][:], ALU.mult)
+            return result
+
+        faded = [fade_tile(m, olds[m]) for m in range(2)]
+
+        for r in range(PACK):
+            nc.vector.scalar_tensor_tensor(
+                parts[r][:], sigs[r][:], rest_col[:, r : r + 1], shared[r][:], ALU.mult, ALU.add, accum_out=sums[r][:]
+            )
+        for r in range(PACK):
+            nc.vector.reciprocal(inverse[r][:], sums[r][:])
+        for r in range(PACK):
+            nc.vector.tensor_scalar(
+                weights[:, r], parts[r][:], inverse[r][:], qs_col[:, r : r + 1], ALU.mult, ALU.mult
+            )
+
+        grows_bf = keep.tile([P, E, PACK], BF16, name="grows_bf", tag="late3", align_bytes=64)
+        grows_codes = keep.tile([P, E], U32, name="grows_codes", align_bytes=64)
+        grows_scales = keep.tile([P, E], U8, name="grows_scales", align_bytes=64)
+        for m in range(tiles_e):
+            cols = slice(m * P, (m + 1) * P)
+            nc.scalar.copy(
+                grows_bf[:, cols].rearrange("p (c u) j -> p c j u", u=4),
+                grows_raw[:, :, cols].rearrange("p j (c u) -> p c j u", u=4),
+            )
+
+        weights_woven = keep.tile([P, I, PACK], BF16, name="weights_woven", tag="late2", align_bytes=64)
+        nc.vector.tensor_copy(
+            weights_woven[:].rearrange("p (c u) r -> p c r u", u=4),
+            weights[:].rearrange("p r (c u) -> p c r u", u=4),
+        )
+
+        def quantize_grows(m):
+            cols = slice(m * P, (m + 1) * P)
+            nc.vector.quantize_mx(
+                out=grows_codes[:, cols].bitcast(FP8X4),
+                scales=grows_scales[:, cols],
+                in_=grows_bf[:, cols].rearrange("p e j -> p (e j)"),
+            )
+
+        quantize_grows(0)
+        weight_codes = keep.tile([P, I], U32, name="weight_codes", align_bytes=64)
+        weight_scales = keep.tile([P, I], U8, name="weight_scales", align_bytes=64)
+        nc.vector.quantize_mx(
+            out=weight_codes[:].bitcast(FP8X4),
+            scales=weight_scales[:],
+            in_=weights_woven[:].rearrange("p i r -> p (i r)"),
+        )
+        for m in range(1, tiles_e):
+            quantize_grows(m)
+
+        values = [keep.tile([P, I], F32, name=f"values{m}") for m in range(tiles_e)]
+        for m in range(tiles_e):
+            cols = slice(m * P, (m + 1) * P)
+            product = psum.tile([P, I], F32, name=f"product{m}", tag=f"bank{m}")
+            nc.tensor.matmul_mx(
+                out=product[:],
+                lhsT=grows_codes[:, cols].bitcast(FP8X4),
+                lhsT_scale=grows_scales[:, cols],
+                rhs=weight_codes[:].bitcast(FP8X4),
+                rhs_scale=weight_scales[:],
+                start=True,
+                stop=True,
+            )
+            if m == 0:
+                nc.scalar.copy(values[m][:], product[:])
+            else:
+                nc.vector.tensor_copy(values[m][:], product[:])
+            nc.scalar.activation(placed[m][:].indirect(offsets[:]), values[m][:], ACT.Copy)
+
+        for m in range(2, tiles_e):
+            faded.append(fade_tile(m, keep.tile([P, T], F32, name=f"faded{m}", tag=f"late{m}", align_bytes=64)))
+        for m in range(tiles_e):
+            width = T if m < tiles_e - 1 else T // 2
+            for start in range(0, T, width):
+                cols = slice(start, start + width)
+                nc.vector.tensor_tensor(faded[m][:, cols], faded[m][:, cols], placed[m][:, cols], ALU.add)
+                nc.sync.dma_start(out[m * P : (m + 1) * P, cols], faded[m][:, cols])

@@ -19,7 +19,6 @@ ALU = mybir.AluOpType
 P = 128
 PACK = 4
 BANK = 512
-QUERY_SPLIT = 84
 
 
 def tile_attend_bmixedparts_v_kernel(tc, query, keys_words, keys_scales, share, qs, grows, old, fade, offs, out):
@@ -34,9 +33,8 @@ def tile_attend_bmixedparts_v_kernel(tc, query, keys_words, keys_scales, share, 
 
         pool_words = keep.tile([P, T], U32, name="pool_words", align_bytes=64)
         pool_scales = keep.tile([P, T], U8, name="pool_scales", align_bytes=64)
-        fade_rows = keep.tile([P, P], F32, name="fade_rows")
+        fade_cols = keep.tile([P, T // BANK, PACK], F32, name="fade_cols")
         nc.gpsimd.memset(pool_scales[:].bitcast(I32), 0)
-        nc.gpsimd.memset(fade_rows[:], 0.0)
 
         nc.sync.dma_start(pool_words[:].bitcast(I32), keys_words[0].rearrange("p n t -> p (n t)").bitcast(I32))
         for quad in range(4):
@@ -44,7 +42,7 @@ def tile_attend_bmixedparts_v_kernel(tc, query, keys_words, keys_scales, share, 
                 pool_scales[32 * quad : 32 * quad + 4, :].bitcast(I32),
                 keys_scales[0, 4 * quad : 4 * quad + 4, :].bitcast(I32),
             )
-        nc.sync.dma_start(fade_rows[0 : T // P, :], fade.rearrange("o (k n) -> (o k) n", n=P))
+        nc.scalar.dma_start(fade_cols[:], fade.rearrange("o (h n k) -> n (o h) k", n=P, k=PACK))
         query_raw = keep.tile([P, PACK, Q], F32, name="query_raw")
         nc.sync.dma_start(query_raw[:], query.rearrange("(p j) q -> p j q", j=PACK))
         share_col = keep.tile([P, PACK], F32, name="share_col")
@@ -54,10 +52,10 @@ def tile_attend_bmixedparts_v_kernel(tc, query, keys_words, keys_scales, share, 
 
         olds = [keep.tile([P, T], F32, name=f"olds{m}") for m in range(tiles_e)]
         grows_raw = keep.tile([P, PACK, E], F32, name="grows_raw")
-        for m in range(2):
+        for m in range(3):
             nc.sync.dma_start(olds[m][:], old[m * P : (m + 1) * P, :])
         nc.sync.dma_start(grows_raw[:], grows.rearrange("(p j) e -> p j e", j=PACK))
-        for m in range(2, tiles_e):
+        for m in range(3, tiles_e):
             nc.sync.dma_start(olds[m][:], old[m * P : (m + 1) * P, :])
 
         identity = keep.tile([P, P], F32, name="identity")
@@ -66,31 +64,24 @@ def tile_attend_bmixedparts_v_kernel(tc, query, keys_words, keys_scales, share, 
         for m in range(tiles_e):
             nc.vector.memset(placed[m][:], 0.0)
 
-        rest_col = keep.tile([P, PACK], F32, name="rest_col")
-        nc.scalar.activation(rest_col[:], share_col[:], ACT.Copy, bias=3.0, scale=-3.0)
+        fade_wide = [psum.tile([P, PACK, P], F32, name=f"fade_wide{h}") for h in range(T // BANK)]
+        for h in range(T // BANK):
+            for k in range(PACK):
+                nc.tensor.transpose(fade_wide[h][:, k], fade_cols[:, h, k : k + 1].to_broadcast([P, P]), identity[:])
 
-        fade_turned = psum.tile([P, P], F32, name="fade_turned")
-        nc.tensor.transpose(fade_turned[:], fade_rows[:], identity[:])
-        fade_cols = keep.tile([P, T // P], F32, name="fade_cols")
-        nc.scalar.copy(fade_cols[:], fade_turned[:, 0 : T // P])
-        fade_wide = [psum.tile([P, BANK], F32, name=f"fade_wide{h}") for h in range(T // BANK)]
-        for k in range(T // P):
-            nc.tensor.transpose(
-                fade_wide[k // 4][:, (k % 4) * P : (k % 4 + 1) * P],
-                fade_cols[:, k : k + 1].to_broadcast([P, P]),
-                identity[:],
-            )
+        fade_flat = keep.tile([P, P, PACK], F32, name="fade_flat")
+        nc.scalar.copy(fade_flat[:], fade_wide[0][:].rearrange("p k n -> p n k"))
 
         key_words = keep.tile([P, I], U32, name="key_words", align_bytes=64)
         key_scales = keep.tile([P, I], U8, name="key_scales", align_bytes=64)
         nc.vector.tensor_copy(key_words[:], pool_words[:].indirect(offsets[:]))
         nc.vector.tensor_copy(key_scales[:], pool_scales[:].indirect(offsets[:]))
 
-        query_bf = keep.tile([P, PACK, P, PACK], BF16, name="query_bf", align_bytes=64)
+        query_bf = keep.tile([P, PACK, P, PACK], BF16, name="query_bf", tag="early0", align_bytes=64)
         dealt_out = query_bf[:].rearrange("p r s j -> p s j r")
         dealt_in = query_raw[:].rearrange("p j (s r) -> p s j r", r=PACK)
-        nc.vector.tensor_copy(dealt_out[:, 0:QUERY_SPLIT], dealt_in[:, 0:QUERY_SPLIT])
-        nc.scalar.copy(dealt_out[:, QUERY_SPLIT:P], dealt_in[:, QUERY_SPLIT:P])
+        nc.vector.tensor_copy(dealt_out[:, :, :, 0:2], dealt_in[:, :, :, 0:2])
+        nc.scalar.activation(dealt_out[:, :, :, 2:4], dealt_in[:, :, :, 2:4], ACT.Copy)
 
         query_codes = keep.tile([P, Q], U32, name="query_codes", align_bytes=64)
         query_scales = keep.tile([P, Q], U8, name="query_scales", align_bytes=64)
@@ -114,31 +105,39 @@ def tile_attend_bmixedparts_v_kernel(tc, query, keys_words, keys_scales, share, 
             )
             scores.append(score)
 
-        exps = [keep.tile([P, I], F32, name=f"exps{r}") for r in range(PACK)]
+        exps = keep.tile([P, PACK, I], F32, name="exps", tag="functions")
         shared = [keep.tile([P, I], F32, name=f"shared{r}") for r in range(PACK)]
-        sigs = [keep.tile([P, I], F32, name=f"sigs{r}") for r in range(PACK)]
         parts = [keep.tile([P, I], F32, name=f"parts{r}") for r in range(PACK)]
         sums = [keep.tile([P, 1], F32, name=f"sums{r}") for r in range(PACK)]
         inverse = [keep.tile([P, 1], F32, name=f"inverse{r}") for r in range(PACK)]
         weights = keep.tile([P, PACK, I], BF16, name="weights")
         for r in range(PACK):
-            nc.scalar.activation(exps[r][:], scores[r][:], ACT.Exp)
+            nc.scalar.activation(exps[:, r], scores[r][:], ACT.Exp)
         for r in range(PACK):
-            nc.scalar.activation(sigs[r][:], scores[r][:], ACT.Sigmoid)
+            nc.gpsimd.tensor_scalar(shared[r][:], exps[:, r], share_col[:, r : r + 1], 0.0, ALU.mult, ALU.add)
+        rest_col = keep.tile([P, PACK], F32, name="rest_col")
+        nc.vector.tensor_scalar(rest_col[:], share_col[:], -3.0, 3.0, ALU.mult, ALU.add)
+        sigs = keep.tile([P, PACK, I], F32, name="sigs", tag="functions")
         for r in range(PACK):
-            nc.vector.tensor_scalar(shared[r][:], exps[r][:], share_col[:, r : r + 1], None, ALU.mult)
+            nc.scalar.activation(sigs[:, r], scores[r][:], ACT.Sigmoid)
 
-        def fade_tile(m, result):
-            for h in range(T // BANK):
+        def fade_tile(m, result, first=0):
+            for h in range(first, T // BANK):
                 cols = slice(h * BANK, (h + 1) * BANK)
-                nc.vector.tensor_tensor(result[:, cols], olds[m][:, cols], fade_wide[h][:], ALU.mult)
+                nc.vector.tensor_tensor(
+                    result[:, cols].rearrange("p (n k) -> p n k", k=PACK),
+                    olds[m][:, cols].rearrange("p (n k) -> p n k", k=PACK),
+                    fade_wide[h][:].rearrange("p k n -> p n k"),
+                    ALU.mult,
+                )
             return result
 
-        faded = [fade_tile(m, olds[m]) for m in range(2)]
+        faded = [fade_tile(0, keep.tile([P, T], F32, name="faded0", tag="early0", align_bytes=64))]
+        faded.extend(fade_tile(m, olds[m]) for m in range(1, 3))
 
         for r in range(PACK):
             nc.vector.scalar_tensor_tensor(
-                parts[r][:], sigs[r][:], rest_col[:, r : r + 1], shared[r][:], ALU.mult, ALU.add, accum_out=sums[r][:]
+                parts[r][:], sigs[:, r], rest_col[:, r : r + 1], shared[r][:], ALU.mult, ALU.add, accum_out=sums[r][:]
             )
         for r in range(PACK):
             nc.vector.reciprocal(inverse[r][:], sums[r][:])
@@ -148,7 +147,6 @@ def tile_attend_bmixedparts_v_kernel(tc, query, keys_words, keys_scales, share, 
             )
 
         grows_bf = keep.tile([P, E, PACK], BF16, name="grows_bf", tag="late3", align_bytes=64)
-        grows_codes = keep.tile([P, E], U32, name="grows_codes", align_bytes=64)
         grows_scales = keep.tile([P, E], U8, name="grows_scales", align_bytes=64)
         for m in range(tiles_e):
             cols = slice(m * P, (m + 1) * P)
@@ -157,55 +155,74 @@ def tile_attend_bmixedparts_v_kernel(tc, query, keys_words, keys_scales, share, 
                 grows_raw[:, :, cols].rearrange("p j (c u) -> p c j u", u=4),
             )
 
-        weights_woven = keep.tile([P, I, PACK], BF16, name="weights_woven", tag="late2", align_bytes=64)
-        nc.vector.tensor_copy(
-            weights_woven[:].rearrange("p (c u) r -> p c r u", u=4),
-            weights[:].rearrange("p r (c u) -> p c r u", u=4),
-        )
-
-        def quantize_grows(m):
-            cols = slice(m * P, (m + 1) * P)
+        def quantize_grows(pair, tag):
+            cols = slice(pair * 2 * P, (pair + 1) * 2 * P)
+            codes = keep.tile([P, 2 * P], U32, name=f"grows_codes{pair}", tag=tag, align_bytes=64)
+            grows_codes.append(codes)
             nc.vector.quantize_mx(
-                out=grows_codes[:, cols].bitcast(FP8X4),
+                out=codes[:].bitcast(FP8X4),
                 scales=grows_scales[:, cols],
                 in_=grows_bf[:, cols].rearrange("p e j -> p (e j)"),
             )
 
-        quantize_grows(0)
+        grows_codes = []
+        quantize_grows(0, "first_codes")
+        half = I // 2
+        halves = [slice(0, half), slice(half, I)]
+        weights_woven = keep.tile([P, I, PACK], BF16, name="weights_woven", tag="woven", align_bytes=64)
         weight_codes = keep.tile([P, I], U32, name="weight_codes", align_bytes=64)
         weight_scales = keep.tile([P, I], U8, name="weight_scales", align_bytes=64)
-        nc.vector.quantize_mx(
-            out=weight_codes[:].bitcast(FP8X4),
-            scales=weight_scales[:],
-            in_=weights_woven[:].rearrange("p i r -> p (i r)"),
-        )
-        for m in range(1, tiles_e):
-            quantize_grows(m)
+        for slots in halves:
+            nc.vector.tensor_copy(
+                weights_woven[:, slots].rearrange("p (c u) r -> p c r u", u=4),
+                weights[:, :, slots].rearrange("p r (c u) -> p c r u", u=4),
+            )
+        for slots in halves:
+            nc.vector.quantize_mx(
+                out=weight_codes[:, slots].bitcast(FP8X4),
+                scales=weight_scales[:, slots],
+                in_=weights_woven[:, slots].rearrange("p i r -> p (i r)"),
+            )
+        quantize_grows(1, "woven")
 
-        values = [keep.tile([P, I], F32, name=f"values{m}") for m in range(tiles_e)]
-        for m in range(tiles_e):
+        def multiply(m, slots, tag):
             cols = slice(m * P, (m + 1) * P)
-            product = psum.tile([P, I], F32, name=f"product{m}", tag=f"bank{m}")
+            product = psum.tile([P, slots.stop - slots.start], F32, name=f"product{m}_{slots.start}", tag=tag)
             nc.tensor.matmul_mx(
                 out=product[:],
-                lhsT=grows_codes[:, cols].bitcast(FP8X4),
+                lhsT=grows_codes[m // 2][:, (m % 2) * P : (m % 2 + 1) * P].bitcast(FP8X4),
                 lhsT_scale=grows_scales[:, cols],
-                rhs=weight_codes[:].bitcast(FP8X4),
-                rhs_scale=weight_scales[:],
+                rhs=weight_codes[:, slots].bitcast(FP8X4),
+                rhs_scale=weight_scales[:, slots],
                 start=True,
                 stop=True,
             )
-            if m == 0:
-                nc.scalar.copy(values[m][:], product[:])
-            else:
-                nc.vector.tensor_copy(values[m][:], product[:])
-            nc.scalar.activation(placed[m][:].indirect(offsets[:]), values[m][:], ACT.Copy)
+            return product
 
+        def window(m, slots):
+            return placed[m][:].indirect(offsets[:, slots.start // 16 : slots.stop // 16])
+
+        values = [keep.tile([P, I], F32, name=f"values{m}") for m in range(tiles_e)]
+        whole = slice(0, I)
+        for slots, tag in zip(halves, ("bank0", "spare")):
+            nc.scalar.copy(values[0][:, slots], multiply(0, slots, tag)[:])
+            nc.scalar.activation(window(0, slots), values[0][:, slots], ACT.Copy)
+        products = [multiply(m, whole, f"bank{m}") for m in range(1, tiles_e)]
+
+        faded.append(keep.tile([P, T], F32, name="faded3", tag="late3", align_bytes=64))
+        nc.gpsimd.tensor_tensor(
+            faded[3][:, 0:BANK], olds[3][:, 0:BANK], fade_flat[:].rearrange("p n k -> p (n k)"), ALU.mult
+        )
+        nc.vector.tensor_copy(values[1][:], products[0][:])
+        nc.vector.tensor_copy(window(1, halves[0]), values[1][:, halves[0]])
+        nc.scalar.activation(window(1, halves[1]), values[1][:, halves[1]], ACT.Copy)
         for m in range(2, tiles_e):
-            faded.append(fade_tile(m, keep.tile([P, T], F32, name=f"faded{m}", tag=f"late{m}", align_bytes=64)))
+            nc.vector.tensor_copy(values[m][:], products[m - 1][:])
+            nc.scalar.activation(window(m, whole), values[m][:], ACT.Copy)
+        fade_tile(3, faded[3], first=1)
+
         for m in range(tiles_e):
-            width = T if m < tiles_e - 1 else T // 2
-            for start in range(0, T, width):
-                cols = slice(start, start + width)
+            for start in range(0, T, BANK):
+                cols = slice(start, start + BANK)
                 nc.vector.tensor_tensor(faded[m][:, cols], faded[m][:, cols], placed[m][:, cols], ALU.add)
                 nc.sync.dma_start(out[m * P : (m + 1) * P, cols], faded[m][:, cols])

from contextlib import ExitStack

import concourse.mybir as mybir
from concourse.masks import make_identity

D, E, T, I, Q = 512, 512, 1024, 256, 512
FLOPS = 2 * D * Q * I + 2 * Q * E * I

F32 = mybir.dt.float32
BF16 = mybir.dt.bfloat16
I32 = mybir.dt.int32
U32 = mybir.dt.uint32
U16 = mybir.dt.uint16
U8 = mybir.dt.uint8
FP8X4 = mybir.dt.float8_e4m3fn_x4
ACT = mybir.ActivationFunctionType
ALU = mybir.AluOpType

P = 128
PACK = 4
BANK = 512


def tile_attend_bmixedparts_v_kernel(tc, query, keys_words, keys_scales, share, qs, grows, old, fade, offs, out):
    nc = tc.nc
    tiles_e = E // P
    with ExitStack() as ctx:
        keep = ctx.enter_context(tc.tile_pool(name="keep", bufs=1))
        psum = ctx.enter_context(tc.psum_pool(name="psum", bufs=1))

        offsets = keep.tile([P, I // 16], U16, name="offsets")
        nc.sync.dma_start(offsets[:], offs)

        pool_words = keep.tile([P, T], U32, name="pool_words", align_bytes=64)
        pool_scales = keep.tile([P, T], U8, name="pool_scales", align_bytes=64)
        fade_cols = keep.tile([P, T // BANK, PACK], F32, name="fade_cols")
        nc.gpsimd.memset(pool_scales[:].bitcast(I32), 0)

        nc.sync.dma_start(pool_words[:].bitcast(I32), keys_words[0].rearrange("p n t -> p (n t)").bitcast(I32))
        for quad in range(4):
            nc.sync.dma_start(
                pool_scales[32 * quad : 32 * quad + 4, :].bitcast(I32),
                keys_scales[0, 4 * quad : 4 * quad + 4, :].bitcast(I32),
            )
        nc.scalar.dma_start(fade_cols[:], fade.rearrange("o (h n k) -> n (o h) k", n=P, k=PACK))
        query_raw = keep.tile([P, PACK, Q], F32, name="query_raw")
        nc.sync.dma_start(query_raw[:], query.rearrange("(p j) q -> p j q", j=PACK))
        share_col = keep.tile([P, PACK], F32, name="share_col")
        qs_col = keep.tile([P, PACK], F32, name="qs_col")
        nc.sync.dma_start(share_col[:], share.rearrange("(p r) o -> p (r o)", r=PACK))
        nc.sync.dma_start(qs_col[:], qs.rearrange("(p r) o -> p (r o)", r=PACK))

        olds = [keep.tile([P, T], F32, name=f"olds{m}") for m in range(tiles_e)]
        grows_raw = keep.tile([P, PACK, E], F32, name="grows_raw")
        for m in range(3):
            nc.sync.dma_start(olds[m][:], old[m * P : (m + 1) * P, :])
        nc.sync.dma_start(grows_raw[:], grows.rearrange("(p j) e -> p j e", j=PACK))
        for m in range(3, tiles_e):
            nc.sync.dma_start(olds[m][:], old[m * P : (m + 1) * P, :])

        identity = keep.tile([P, P], F32, name="identity")
        make_identity(nc, identity[:])
        placed = [keep.tile([P, T], F32, name=f"placed{m}") for m in range(tiles_e)]
        for m in range(tiles_e):
            nc.vector.memset(placed[m][:], 0.0)

        fade_wide = [psum.tile([P, PACK, P], F32, name=f"fade_wide{h}") for h in range(T // BANK)]
        for h in range(T // BANK):
            for k in range(PACK):
                nc.tensor.transpose(fade_wide[h][:, k], fade_cols[:, h, k : k + 1].to_broadcast([P, P]), identity[:])

        fade_flat = keep.tile([P, P, PACK], F32, name="fade_flat")
        nc.scalar.copy(fade_flat[:], fade_wide[0][:].rearrange("p k n -> p n k"))

        key_words = keep.tile([P, I], U32, name="key_words", align_bytes=64)
        key_scales = keep.tile([P, I], U8, name="key_scales", align_bytes=64)
        nc.vector.tensor_copy(key_words[:], pool_words[:].indirect(offsets[:]))
        nc.vector.tensor_copy(key_scales[:], pool_scales[:].indirect(offsets[:]))

        query_bf = keep.tile([P, PACK, P, PACK], BF16, name="query_bf", tag="early0", align_bytes=64)
        dealt_out = query_bf[:].rearrange("p r s j -> p s j r")
        dealt_in = query_raw[:].rearrange("p j (s r) -> p s j r", r=PACK)
        nc.vector.tensor_copy(dealt_out[:, :, :, 0:2], dealt_in[:, :, :, 0:2])
        nc.scalar.activation(dealt_out[:, :, :, 2:4], dealt_in[:, :, :, 2:4], ACT.Copy)

        query_codes = keep.tile([P, Q], U32, name="query_codes", align_bytes=64)
        query_scales = keep.tile([P, Q], U8, name="query_scales", align_bytes=64)
        scores = []
        for r in range(PACK):
            cols = slice(r * P, (r + 1) * P)
            nc.vector.quantize_mx(
                out=query_codes[:, cols].bitcast(FP8X4),
                scales=query_scales[:, cols],
                in_=query_bf[:, r].rearrange("p s j -> p (s j)"),
            )
            score = psum.tile([P, I], F32, name=f"score{r}", tag=f"bank{r}")
            nc.tensor.matmul_mx(
                out=score[:],
                lhsT=query_codes[:, cols].bitcast(FP8X4),
                lhsT_scale=query_scales[:, cols],
                rhs=key_words[:].bitcast(FP8X4),
                rhs_scale=key_scales[:],
                start=True,
                stop=True,
            )
            scores.append(score)

        exps = keep.tile([P, PACK, I], F32, name="exps", tag="functions")
        shared = [keep.tile([P, I], F32, name=f"shared{r}") for r in range(PACK)]
        parts = [keep.tile([P, I], F32, name=f"parts{r}") for r in range(PACK)]
        sums = [keep.tile([P, 1], F32, name=f"sums{r}") for r in range(PACK)]
        inverse = [keep.tile([P, 1], F32, name=f"inverse{r}") for r in range(PACK)]
        weights = keep.tile([P, PACK, I], BF16, name="weights")
        for r in range(PACK):
            nc.scalar.activation(exps[:, r], scores[r][:], ACT.Exp)
        for r in range(PACK):
            nc.gpsimd.tensor_scalar(shared[r][:], exps[:, r], share_col[:, r : r + 1], 0.0, ALU.mult, ALU.add)
        rest_col = keep.tile([P, PACK], F32, name="rest_col")
        nc.vector.tensor_scalar(rest_col[:], share_col[:], -3.0, 3.0, ALU.mult, ALU.add)
        sigs = keep.tile([P, PACK, I], F32, name="sigs", tag="functions")
        for r in range(PACK):
            nc.scalar.activation(sigs[:, r], scores[r][:], ACT.Sigmoid)

        def fade_tile(m, result, first=0):
            for h in range(first, T // BANK):
                cols = slice(h * BANK, (h + 1) * BANK)
                nc.vector.tensor_tensor(
                    result[:, cols].rearrange("p (n k) -> p n k", k=PACK),
                    olds[m][:, cols].rearrange("p (n k) -> p n k", k=PACK),
                    fade_wide[h][:].rearrange("p k n -> p n k"),
                    ALU.mult,
                )
            return result

        faded = [fade_tile(0, keep.tile([P, T], F32, name="faded0", tag="early0", align_bytes=64))]
        faded.extend(fade_tile(m, olds[m]) for m in range(1, 3))

        for r in range(PACK):
            nc.vector.scalar_tensor_tensor(
                parts[r][:], sigs[:, r], rest_col[:, r : r + 1], shared[r][:], ALU.mult, ALU.add, accum_out=sums[r][:]
            )
        for r in range(PACK):
            nc.vector.reciprocal(inverse[r][:], sums[r][:])
        for r in range(PACK):
            nc.vector.tensor_scalar(
                weights[:, r], parts[r][:], inverse[r][:], qs_col[:, r : r + 1], ALU.mult, ALU.mult
            )

        grows_bf = keep.tile([P, E, PACK], BF16, name="grows_bf", tag="late3", align_bytes=64)
        grows_scales = keep.tile([P, E], U8, name="grows_scales", align_bytes=64)
        for m in range(tiles_e):
            cols = slice(m * P, (m + 1) * P)
            nc.scalar.copy(
                grows_bf[:, cols].rearrange("p (c u) j -> p c j u", u=4),
                grows_raw[:, :, cols].rearrange("p j (c u) -> p c j u", u=4),
            )

        def quantize_grows(pair, tag):
            cols = slice(pair * 2 * P, (pair + 1) * 2 * P)
            codes = keep.tile([P, 2 * P], U32, name=f"grows_codes{pair}", tag=tag, align_bytes=64)
            grows_codes.append(codes)
            nc.vector.quantize_mx(
                out=codes[:].bitcast(FP8X4),
                scales=grows_scales[:, cols],
                in_=grows_bf[:, cols].rearrange("p e j -> p (e j)"),
            )

        grows_codes = []
        quantize_grows(0, "first_codes")
        half = I // 2
        halves = [slice(0, half), slice(half, I)]
        weights_woven = keep.tile([P, I, PACK], BF16, name="weights_woven", tag="woven", align_bytes=64)
        weight_codes = keep.tile([P, I], U32, name="weight_codes", align_bytes=64)
        weight_scales = keep.tile([P, I], U8, name="weight_scales", align_bytes=64)
        for slots in halves:
            nc.vector.tensor_copy(
                weights_woven[:, slots].rearrange("p (c u) r -> p c r u", u=4),
                weights[:, :, slots].rearrange("p r (c u) -> p c r u", u=4),
            )
        for slots in halves:
            nc.vector.quantize_mx(
                out=weight_codes[:, slots].bitcast(FP8X4),
                scales=weight_scales[:, slots],
                in_=weights_woven[:, slots].rearrange("p i r -> p (i r)"),
            )
        quantize_grows(1, "woven")

        def multiply(m, slots, tag):
            cols = slice(m * P, (m + 1) * P)
            product = psum.tile([P, slots.stop - slots.start], F32, name=f"product{m}_{slots.start}", tag=tag)
            nc.tensor.matmul_mx(
                out=product[:],
                lhsT=grows_codes[m // 2][:, (m % 2) * P : (m % 2 + 1) * P].bitcast(FP8X4),
                lhsT_scale=grows_scales[:, cols],
                rhs=weight_codes[:, slots].bitcast(FP8X4),
                rhs_scale=weight_scales[:, slots],
                start=True,
                stop=True,
            )
            return product

        def window(m, slots):
            return placed[m][:].indirect(offsets[:, slots.start // 16 : slots.stop // 16])

        values = [keep.tile([P, I], F32, name=f"values{m}") for m in range(tiles_e)]
        whole = slice(0, I)
        for slots, tag in zip(halves, ("bank0", "spare")):
            nc.scalar.copy(values[0][:, slots], multiply(0, slots, tag)[:])
            nc.scalar.activation(window(0, slots), values[0][:, slots], ACT.Copy)
        products = [multiply(m, whole, f"bank{m}") for m in range(1, tiles_e)]

        faded.append(keep.tile([P, T], F32, name="faded3", tag="late3", align_bytes=64))
        nc.gpsimd.tensor_tensor(
            faded[3][:, 0:BANK], olds[3][:, 0:BANK], fade_flat[:].rearrange("p n k -> p (n k)"), ALU.mult
        )
        nc.vector.tensor_copy(values[1][:], products[0][:])
        nc.vector.tensor_copy(window(1, halves[0]), values[1][:, halves[0]])
        nc.scalar.activation(window(1, halves[1]), values[1][:, halves[1]], ACT.Copy)
        for m in range(2, tiles_e):
            nc.vector.tensor_copy(values[m][:], products[m - 1][:])
            nc.scalar.activation(window(m, whole), values[m][:], ACT.Copy)
        fade_tile(3, faded[3], first=1)

        for m in range(tiles_e):
            for start in range(0, T, BANK):
                cols = slice(start, start + BANK)
                nc.vector.tensor_tensor(faded[m][:, cols], faded[m][:, cols], placed[m][:, cols], ALU.add)
                nc.sync.dma_start(out[m * P : (m + 1) * P, cols], faded[m][:, cols])
